import numpy as np
import ml_dtypes

BF16 = ml_dtypes.bfloat16


def bf(x):
    return np.asarray(x, np.float32).astype(BF16)


def f32(x):
    return np.asarray(x, np.float32)


def f64(x):
    return np.asarray(x).astype(np.float64)


def striped(idx):
    return np.tile(idx.reshape(-1, 16).T, (8, 1))


S, K, M, N, T, D = 256, 128, 384, 128, 512, 256


def setup_inputs():
    return {"base": bf(np.random.standard_normal((M, S))), "q": bf(1.5 * np.random.standard_normal((K, N)) / np.sqrt(K)), "k": bf(np.random.standard_normal((K, T))), "v": bf(np.random.standard_normal((T, D))), "w": bf(2.0 * np.random.standard_normal((D, M)) / np.sqrt(D)), "r": f32(0.7 * np.random.standard_normal((1, T))), "offs": striped(np.random.permutation(S)[:N])}


def reference(base, q, k, v, w, r, offs):
    idx = offs[:16].T.reshape(-1)
    a = f64(q).T @ f64(k) + f64(r)
    a = np.exp(a - a.max(axis=1, keepdims=True))
    a = a / a.sum(axis=1, keepdims=True)
    z = f64(base).copy()
    z[:, idx] += f64(w).T @ (a @ f64(v)).T
    return z

@@ -1,0 +1,87 @@
+import concourse.mybir as mybir
+from concourse.masks import make_identity
+
+P = 128
+S, K, M, N, T, D = 256, 128, 384, 128, 512, 256
+T_BLOCKS, D_BLOCKS, M_BLOCKS = T // P, D // P, M // P
+BF16, F32, U16 = mybir.dt.bfloat16, mybir.dt.float32, mybir.dt.uint16
+FLOPS = 2 * N * (K * T + T * D + D * M)
+
+
+def tile_rows_attnback_kernel(tc, base, q, k, v, w, r, offs, out):
+    nc = tc.nc
+    mult, Exp = mybir.AluOpType.mult, mybir.ActivationFunctionType.Exp
+    with (
+        tc.tile_pool(name="held", bufs=1) as held,
+        tc.psum_pool(name="psum", bufs=1) as psum,
+    ):
+        r_row = held.tile([1, T], F32, name="r_row")
+        nc.sync.dma_start(r_row[:], r)
+        q_in = held.tile([K, N], BF16, name="q_in")
+        nc.sync.dma_start(q_in[:], q)
+        k_in = held.tile([K, T], BF16, name="k_in")
+        nc.sync.dma_start(k_in[:], k)
+        base_in = held.tile([P, M_BLOCKS, S], BF16, name="base_in")
+        nc.sync.dma_start(base_in[:], base.rearrange("(a p) s -> p a s", p=P))
+        v_in = held.tile([P, T_BLOCKS, D], BF16, name="v_in")
+        nc.sync.dma_start(v_in[:], v.rearrange("(a p) d -> p a d", p=P))
+        w_in = held.tile([P, D_BLOCKS, M], BF16, name="w_in")
+        nc.sync.dma_start(w_in[:], w.rearrange("(a p) m -> p a m", p=P))
+        offsets = held.tile([P, N // 16], U16, name="offsets")
+        nc.sync.dma_start(offsets[:], offs)
+
+        ident = held.tile([P, P], BF16, name="ident")
+        make_identity(nc, ident[:])
+        ones_row = held.tile([1, N], F32, name="ones_row")
+        nc.vector.memset(ones_row[:], 1.0)
+        ones = held.tile([P, P], BF16, name="ones")
+        nc.vector.memset(ones[:], 1.0)
+
+        scores = psum.tile([N, T], F32, name="scores")
+        nc.tensor.matmul(scores[:], ones_row[:], r_row[:], start=True, stop=False)
+        nc.tensor.matmul(scores[:], q_in[:], k_in[:], start=False, stop=True)
+
+        windows = [psum.tile([P, S], F32, name=f"window{m}") for m in range(M_BLOCKS)]
+        for m in range(M_BLOCKS):
+            nc.tensor.matmul(windows[m][:], ident[:], base_in[:, m, :], start=True, stop=False)
+
+        neg_max = held.tile([N, 1], F32, name="neg_max")
+        nc.vector.reduce_max(neg_max[:], scores[:], axis=mybir.AxisListType.X, negate=True)
+        e = held.tile([N, T], BF16, name="e")
+        nc.scalar.activation(e[:], scores[:], Exp, bias=neg_max[:])
+
+        e_t_psum = psum.tile([P, T_BLOCKS, N], BF16, name="e_t_psum")
+        for t in range(T_BLOCKS):
+            nc.tensor.transpose(e_t_psum[:, t, :], e[:, t * P : (t + 1) * P], ident[:])
+        e_t = held.tile([P, T_BLOCKS, N], BF16, name="e_t")
+        nc.vector.tensor_copy(e_t[:], e_t_psum[:])
+
+        sums = psum.tile([P, N], F32, name="sums")
+        for t in range(T_BLOCKS):
+            nc.tensor.matmul(sums[:], ones[:], e_t[:, t, :], start=t == 0, stop=t == T_BLOCKS - 1)
+        inverse = held.tile([P, N], F32, name="inverse")
+        nc.vector.reciprocal(inverse[:], sums[:])
+
+        o_t = [held.tile([P, N], BF16, name=f"o_t{d}") for d in range(D_BLOCKS)]
+        for d in range(D_BLOCKS):
+            o_psum = psum.tile([P, N], F32, name=f"o_psum{d}")
+            for t in range(T_BLOCKS):
+                nc.tensor.matmul(
+                    o_psum[:], v_in[:, t, d * P : (d + 1) * P], e_t[:, t, :], start=t == 0, stop=t == T_BLOCKS - 1
+                )
+            nc.vector.tensor_tensor(o_t[d][:], o_psum[:], inverse[:], mult)
+
+        for d in range(D_BLOCKS):
+            for m in range(M_BLOCKS):
+                nc.tensor.matmul(
+                    windows[m][:].indirect(offsets[:]),
+                    w_in[:, d, m * P : (m + 1) * P],
+                    o_t[d][:],
+                    start=False,
+                    stop=d == D_BLOCKS - 1,
+                )
+
+        for m in range(M_BLOCKS):
+            z = held.tile([P, S], F32, name=f"z{m}")
+            nc.vector.tensor_copy(z[:], windows[m][:])
+            nc.sync.dma_start(out[m * P : (m + 1) * P, :], z[:])

@@ -5,6 +5,9 @@ P = 128
 S, K, M, N, T, D = 256, 128, 384, 128, 512, 256
 T_BLOCKS, D_BLOCKS, M_BLOCKS = T // P, D // P, M // P
 BF16, F32, U16 = mybir.dt.bfloat16, mybir.dt.float32, mybir.dt.uint16
+HALVES = 2
+WARM_UPS = 5
+FILLERS = 3
 FLOPS = 2 * N * (K * T + T * D + D * M)
 
 
@@ -15,12 +18,12 @@ def tile_rows_attnback_kernel(tc, base, q, k, v, w, r, offs, out):
         tc.tile_pool(name="held", bufs=1) as held,
         tc.psum_pool(name="psum", bufs=1) as psum,
     ):
-        r_row = held.tile([1, T], F32, name="r_row")
-        nc.sync.dma_start(r_row[:], r)
+        k_in = held.tile([K, T], BF16, name="k_in")
+        nc.scalar.dma_start(k_in[:], k)
         q_in = held.tile([K, N], BF16, name="q_in")
         nc.sync.dma_start(q_in[:], q)
-        k_in = held.tile([K, T], BF16, name="k_in")
-        nc.sync.dma_start(k_in[:], k)
+        r_in = held.tile([P, T], F32, name="r_in")
+        nc.sync.dma_start(r_in[:], r.rearrange("o t -> (o t)").partition_broadcast(P))
         base_in = held.tile([P, M_BLOCKS, S], BF16, name="base_in")
         nc.sync.dma_start(base_in[:], base.rearrange("(a p) s -> p a s", p=P))
         v_in = held.tile([P, T_BLOCKS, D], BF16, name="v_in")
@@ -30,46 +33,68 @@ def tile_rows_attnback_kernel(tc, base, q, k, v, w, r, offs, out):
         offsets = held.tile([P, N // 16], U16, name="offsets")
         nc.sync.dma_start(offsets[:], offs)
 
+        zeros = held.tile([P, T], BF16, name="zeros")
+        nc.vector.memset(zeros[:], 0.0)
+        warm = psum.tile([P, T], F32, name="warm", tag="spread")
+        for i in range(WARM_UPS):
+            nc.tensor.matmul(warm[:], zeros[:, 0:P], zeros[:], start=True, stop=True)
         ident = held.tile([P, P], BF16, name="ident")
         make_identity(nc, ident[:])
-        ones_row = held.tile([1, N], F32, name="ones_row")
-        nc.vector.memset(ones_row[:], 1.0)
-        ones = held.tile([P, P], BF16, name="ones")
+        ones = held.tile([P, P], F32, name="ones")
         nc.vector.memset(ones[:], 1.0)
 
+        early = held.tile([1, 1], F32, name="early")
+        nc.scalar.activation(early[:], ones[0:1, 0:1], Exp)
+
         scores = psum.tile([N, T], F32, name="scores")
-        nc.tensor.matmul(scores[:], ones_row[:], r_row[:], start=True, stop=False)
-        nc.tensor.matmul(scores[:], q_in[:], k_in[:], start=False, stop=True)
+        nc.tensor.matmul(scores[:], q_in[:], k_in[:], start=True, stop=True)
+
+        for i in range(FILLERS):
+            nc.tensor.matmul(warm[:], q_in[:], k_in[:], start=True, stop=True)
 
         windows = [psum.tile([P, S], F32, name=f"window{m}") for m in range(M_BLOCKS)]
         for m in range(M_BLOCKS):
             nc.tensor.matmul(windows[m][:], ident[:], base_in[:, m, :], start=True, stop=False)
 
+        a = held.tile([N, T], F32, name="a")
+        nc.vector.tensor_tensor(a[:], scores[:], r_in[:], mybir.AluOpType.add)
         neg_max = held.tile([N, 1], F32, name="neg_max")
-        nc.vector.reduce_max(neg_max[:], scores[:], axis=mybir.AxisListType.X, negate=True)
-        e = held.tile([N, T], BF16, name="e")
-        nc.scalar.activation(e[:], scores[:], Exp, bias=neg_max[:])
+        nc.vector.reduce_max(neg_max[:], a[:], axis=mybir.AxisListType.X, negate=True)
+        sums = held.tile([N, HALVES], F32, name="sums")
+        e_t = []
+        for h in range(HALVES):
+            e = held.tile([N, T // HALVES], BF16, name=f"e{h}")
+            nc.scalar.activation(
+                e[:], a[:, h * T // HALVES : (h + 1) * T // HALVES], Exp, bias=neg_max[:], accum_out=sums[:, h : h + 1]
+            )
+            e_t_psum = psum.tile([P, T_BLOCKS // HALVES, N], BF16, name=f"e_t_psum{h}")
+            for t in range(T_BLOCKS // HALVES):
+                nc.tensor.transpose(e_t_psum[:, t, :], e[:, t * P : (t + 1) * P], ident[:])
+            for i in range(2):
+                nc.tensor.matmul(warm[:, 0 : T // HALVES], ident[:], e[:], start=True, stop=True)
+            e_t_half = held.tile([P, T_BLOCKS // HALVES, N], BF16, name=f"e_t{h}")
+            nc.vector.tensor_copy(e_t_half[:], e_t_psum[:])
+            e_t += [e_t_half[:, t, :] for t in range(T_BLOCKS // HALVES)]
 
-        e_t_psum = psum.tile([P, T_BLOCKS, N], BF16, name="e_t_psum")
-        for t in range(T_BLOCKS):
-            nc.tensor.transpose(e_t_psum[:, t, :], e[:, t * P : (t + 1) * P], ident[:])
-        e_t = held.tile([P, T_BLOCKS, N], BF16, name="e_t")
-        nc.vector.tensor_copy(e_t[:], e_t_psum[:])
-
-        sums = psum.tile([P, N], F32, name="sums")
-        for t in range(T_BLOCKS):
-            nc.tensor.matmul(sums[:], ones[:], e_t[:, t, :], start=t == 0, stop=t == T_BLOCKS - 1)
-        inverse = held.tile([P, N], F32, name="inverse")
-        nc.vector.reciprocal(inverse[:], sums[:])
+        total = held.tile([N, 1], F32, name="total")
+        nc.vector.reduce_sum(total[:], sums[:], axis=mybir.AxisListType.X)
+        inverse = held.tile([N, 1], F32, name="inverse")
+        nc.vector.reciprocal(inverse[:], total[:])
+        diagonal = held.tile([N, N], F32, name="diagonal")
+        nc.vector.tensor_scalar(diagonal[:], ident[:], inverse[:], None, mult)
+        spread_psum = psum.tile([P, N], F32, name="spread_psum", tag="e_t_psum0")
+        nc.tensor.matmul(spread_psum[:], ones[:], diagonal[:], start=True, stop=True)
+        spread = held.tile([P, N], F32, name="spread")
+        nc.scalar.copy(spread[:], spread_psum[:])
 
         o_t = [held.tile([P, N], BF16, name=f"o_t{d}") for d in range(D_BLOCKS)]
         for d in range(D_BLOCKS):
-            o_psum = psum.tile([P, N], F32, name=f"o_psum{d}")
+            o_psum = psum.tile([P, N], F32, name=f"o_psum{d}", tag="scores" if d == 0 else "o")
             for t in range(T_BLOCKS):
                 nc.tensor.matmul(
-                    o_psum[:], v_in[:, t, d * P : (d + 1) * P], e_t[:, t, :], start=t == 0, stop=t == T_BLOCKS - 1
+                    o_psum[:], v_in[:, t, d * P : (d + 1) * P], e_t[t], start=t == 0, stop=t == T_BLOCKS - 1
                 )
-            nc.vector.tensor_tensor(o_t[d][:], o_psum[:], inverse[:], mult)
+            nc.vector.tensor_tensor(o_t[d][:], o_psum[:], spread[:], mult)
 
         for d in range(D_BLOCKS):
             for m in range(M_BLOCKS):
@@ -83,5 +108,9 @@ def tile_rows_attnback_kernel(tc, base, q, k, v, w, r, offs, out):
 
         for m in range(M_BLOCKS):
             z = held.tile([P, S], F32, name=f"z{m}")
-            nc.vector.tensor_copy(z[:], windows[m][:])
-            nc.sync.dma_start(out[m * P : (m + 1) * P, :], z[:])
+            if m % 2 == 0:
+                nc.vector.tensor_copy(z[:], windows[m][:])
+                nc.sync.dma_start(out[m * P : (m + 1) * P, :], z[:])
+            else:
+                nc.scalar.copy(z[:], windows[m][:])
+                nc.scalar.dma_start(out[m * P : (m + 1) * P, :], z[:])

@@ -6,7 +6,7 @@ S, K, M, N, T, D = 256, 128, 384, 128, 512, 256
 T_BLOCKS, D_BLOCKS, M_BLOCKS = T // P, D // P, M // P
 BF16, F32, U16 = mybir.dt.bfloat16, mybir.dt.float32, mybir.dt.uint16
 HALVES = 2
-WARM_UPS = 5
+WARM_UPS = 3
 FILLERS = 3
 FLOPS = 2 * N * (K * T + T * D + D * M)
 
@@ -18,12 +18,12 @@ def tile_rows_attnback_kernel(tc, base, q, k, v, w, r, offs, out):
         tc.tile_pool(name="held", bufs=1) as held,
         tc.psum_pool(name="psum", bufs=1) as psum,
     ):
+        r_row = held.tile([1, T], F32, name="r_row")
+        nc.sync.dma_start(r_row[:], r)
         k_in = held.tile([K, T], BF16, name="k_in")
-        nc.scalar.dma_start(k_in[:], k)
+        nc.sync.dma_start(k_in[:], k)
         q_in = held.tile([K, N], BF16, name="q_in")
         nc.sync.dma_start(q_in[:], q)
-        r_in = held.tile([P, T], F32, name="r_in")
-        nc.sync.dma_start(r_in[:], r.rearrange("o t -> (o t)").partition_broadcast(P))
         base_in = held.tile([P, M_BLOCKS, S], BF16, name="base_in")
         nc.sync.dma_start(base_in[:], base.rearrange("(a p) s -> p a s", p=P))
         v_in = held.tile([P, T_BLOCKS, D], BF16, name="v_in")
@@ -47,7 +47,8 @@ def tile_rows_attnback_kernel(tc, base, q, k, v, w, r, offs, out):
         nc.scalar.activation(early[:], ones[0:1, 0:1], Exp)
 
         scores = psum.tile([N, T], F32, name="scores")
-        nc.tensor.matmul(scores[:], q_in[:], k_in[:], start=True, stop=True)
+        nc.tensor.matmul(scores[:], ones[0:1, :], r_row[:], start=True, stop=False)
+        nc.tensor.matmul(scores[:], q_in[:], k_in[:], start=False, stop=True)
 
         for i in range(FILLERS):
             nc.tensor.matmul(warm[:], q_in[:], k_in[:], start=True, stop=True)
@@ -56,16 +57,14 @@ def tile_rows_attnback_kernel(tc, base, q, k, v, w, r, offs, out):
         for m in range(M_BLOCKS):
             nc.tensor.matmul(windows[m][:], ident[:], base_in[:, m, :], start=True, stop=False)
 
-        a = held.tile([N, T], F32, name="a")
-        nc.vector.tensor_tensor(a[:], scores[:], r_in[:], mybir.AluOpType.add)
         neg_max = held.tile([N, 1], F32, name="neg_max")
-        nc.vector.reduce_max(neg_max[:], a[:], axis=mybir.AxisListType.X, negate=True)
+        nc.vector.reduce_max(neg_max[:], scores[:], axis=mybir.AxisListType.X, negate=True)
         sums = held.tile([N, HALVES], F32, name="sums")
         e_t = []
         for h in range(HALVES):
             e = held.tile([N, T // HALVES], BF16, name=f"e{h}")
             nc.scalar.activation(
-                e[:], a[:, h * T // HALVES : (h + 1) * T // HALVES], Exp, bias=neg_max[:], accum_out=sums[:, h : h + 1]
+                e[:], scores[:, h * T // HALVES : (h + 1) * T // HALVES], Exp, bias=neg_max[:], accum_out=sums[:, h : h + 1]
             )
             e_t_psum = psum.tile([P, T_BLOCKS // HALVES, N], BF16, name=f"e_t_psum{h}")
             for t in range(T_BLOCKS // HALVES):
@@ -110,7 +109,6 @@ def tile_rows_attnback_kernel(tc, base, q, k, v, w, r, offs, out):
             z = held.tile([P, S], F32, name=f"z{m}")
             if m % 2 == 0:
                 nc.vector.tensor_copy(z[:], windows[m][:])
-                nc.sync.dma_start(out[m * P : (m + 1) * P, :], z[:])
             else:
                 nc.scalar.copy(z[:], windows[m][:])
-                nc.scalar.dma_start(out[m * P : (m + 1) * P, :], z[:])
+            nc.sync.dma_start(out[m * P : (m + 1) * P, :], z[:])

import concourse.mybir as mybir
from concourse.masks import make_identity

P = 128
S, K, M, N, T, D = 256, 128, 384, 128, 512, 256
T_BLOCKS, D_BLOCKS, M_BLOCKS = T // P, D // P, M // P
BF16, F32, U16 = mybir.dt.bfloat16, mybir.dt.float32, mybir.dt.uint16
HALVES = 2
WARM_UPS = 3
FILLERS = 3
FLOPS = 2 * N * (K * T + T * D + D * M)


def tile_rows_attnback_kernel(tc, base, q, k, v, w, r, offs, out):
    nc = tc.nc
    mult, Exp = mybir.AluOpType.mult, mybir.ActivationFunctionType.Exp
    with (
        tc.tile_pool(name="held", bufs=1) as held,
        tc.psum_pool(name="psum", bufs=1) as psum,
    ):
        r_row = held.tile([1, T], F32, name="r_row")
        nc.sync.dma_start(r_row[:], r)
        k_in = held.tile([K, T], BF16, name="k_in")
        nc.sync.dma_start(k_in[:], k)
        q_in = held.tile([K, N], BF16, name="q_in")
        nc.sync.dma_start(q_in[:], q)
        base_in = held.tile([P, M_BLOCKS, S], BF16, name="base_in")
        nc.sync.dma_start(base_in[:], base.rearrange("(a p) s -> p a s", p=P))
        v_in = held.tile([P, T_BLOCKS, D], BF16, name="v_in")
        nc.sync.dma_start(v_in[:], v.rearrange("(a p) d -> p a d", p=P))
        w_in = held.tile([P, D_BLOCKS, M], BF16, name="w_in")
        nc.sync.dma_start(w_in[:], w.rearrange("(a p) m -> p a m", p=P))
        offsets = held.tile([P, N // 16], U16, name="offsets")
        nc.sync.dma_start(offsets[:], offs)

        zeros = held.tile([P, T], BF16, name="zeros")
        nc.vector.memset(zeros[:], 0.0)
        warm = psum.tile([P, T], F32, name="warm", tag="spread")
        for i in range(WARM_UPS):
            nc.tensor.matmul(warm[:], zeros[:, 0:P], zeros[:], start=True, stop=True)
        ident = held.tile([P, P], BF16, name="ident")
        make_identity(nc, ident[:])
        ones = held.tile([P, P], F32, name="ones")
        nc.vector.memset(ones[:], 1.0)

        early = held.tile([1, 1], F32, name="early")
        nc.scalar.activation(early[:], ones[0:1, 0:1], Exp)

        scores = psum.tile([N, T], F32, name="scores")
        nc.tensor.matmul(scores[:], ones[0:1, :], r_row[:], start=True, stop=False)
        nc.tensor.matmul(scores[:], q_in[:], k_in[:], start=False, stop=True)

        for i in range(FILLERS):
            nc.tensor.matmul(warm[:], q_in[:], k_in[:], start=True, stop=True)

        windows = [psum.tile([P, S], F32, name=f"window{m}") for m in range(M_BLOCKS)]
        for m in range(M_BLOCKS):
            nc.tensor.matmul(windows[m][:], ident[:], base_in[:, m, :], start=True, stop=False)

        neg_max = held.tile([N, 1], F32, name="neg_max")
        nc.vector.reduce_max(neg_max[:], scores[:], axis=mybir.AxisListType.X, negate=True)
        sums = held.tile([N, HALVES], F32, name="sums")
        e_t = []
        for h in range(HALVES):
            e = held.tile([N, T // HALVES], BF16, name=f"e{h}")
            nc.scalar.activation(
                e[:], scores[:, h * T // HALVES : (h + 1) * T // HALVES], Exp, bias=neg_max[:], accum_out=sums[:, h : h + 1]
            )
            e_t_psum = psum.tile([P, T_BLOCKS // HALVES, N], BF16, name=f"e_t_psum{h}")
            for t in range(T_BLOCKS // HALVES):
                nc.tensor.transpose(e_t_psum[:, t, :], e[:, t * P : (t + 1) * P], ident[:])
            for i in range(2):
                nc.tensor.matmul(warm[:, 0 : T // HALVES], ident[:], e[:], start=True, stop=True)
            e_t_half = held.tile([P, T_BLOCKS // HALVES, N], BF16, name=f"e_t{h}")
            nc.vector.tensor_copy(e_t_half[:], e_t_psum[:])
            e_t += [e_t_half[:, t, :] for t in range(T_BLOCKS // HALVES)]

        total = held.tile([N, 1], F32, name="total")
        nc.vector.reduce_sum(total[:], sums[:], axis=mybir.AxisListType.X)
        inverse = held.tile([N, 1], F32, name="inverse")
        nc.vector.reciprocal(inverse[:], total[:])
        diagonal = held.tile([N, N], F32, name="diagonal")
        nc.vector.tensor_scalar(diagonal[:], ident[:], inverse[:], None, mult)
        spread_psum = psum.tile([P, N], F32, name="spread_psum", tag="e_t_psum0")
        nc.tensor.matmul(spread_psum[:], ones[:], diagonal[:], start=True, stop=True)
        spread = held.tile([P, N], F32, name="spread")
        nc.scalar.copy(spread[:], spread_psum[:])

        o_t = [held.tile([P, N], BF16, name=f"o_t{d}") for d in range(D_BLOCKS)]
        for d in range(D_BLOCKS):
            o_psum = psum.tile([P, N], F32, name=f"o_psum{d}", tag="scores" if d == 0 else "o")
            for t in range(T_BLOCKS):
                nc.tensor.matmul(
                    o_psum[:], v_in[:, t, d * P : (d + 1) * P], e_t[t], start=t == 0, stop=t == T_BLOCKS - 1
                )
            nc.vector.tensor_tensor(o_t[d][:], o_psum[:], spread[:], mult)

        for d in range(D_BLOCKS):
            for m in range(M_BLOCKS):
                nc.tensor.matmul(
                    windows[m][:].indirect(offsets[:]),
                    w_in[:, d, m * P : (m + 1) * P],
                    o_t[d][:],
                    start=False,
                    stop=d == D_BLOCKS - 1,
                )

        for m in range(M_BLOCKS):
            z = held.tile([P, S], F32, name=f"z{m}")
            if m % 2 == 0:
                nc.vector.tensor_copy(z[:], windows[m][:])
            else:
                nc.scalar.copy(z[:], windows[m][:])
            nc.sync.dma_start(out[m * P : (m + 1) * P, :], z[:])
